import numpy as np
import ml_dtypes


def mxq(x, axis, fmt="e4m3"):
    dtype, down = {"e4m3": (ml_dtypes.float8_e4m3fn, 7), "e5m2": (ml_dtypes.float8_e5m2, 14)}[fmt]
    v = np.moveaxis(np.asarray(x, np.float32).astype(ml_dtypes.bfloat16).astype(np.float64), axis, -1)
    blocks = v.reshape(v.shape[:-1] + (-1, 32))
    amax = np.abs(blocks).max(-1, keepdims=True)
    byte = np.maximum(np.where(amax > 0, np.frexp(amax)[1] - 1 + 127, 0) - down, 1)
    scale = np.exp2(byte - 127.0)
    codes = (blocks / scale).astype(np.float32).astype(dtype).astype(np.float64)
    return np.moveaxis((codes * scale).reshape(v.shape), -1, axis)


WIDE = False


def mx_kscale(k):
    if not WIDE:
        return np.ones(k)
    levels = np.array([10, -10, 5, -5, 0])
    if k % 512:
        return np.exp2(np.random.permutation(np.resize(levels, k // 32))).repeat(32)
    a = np.empty((k // 512, 16))
    for p in range(k // 512):
        a[p, :8] = np.random.permutation(np.resize(levels, 8))
        for g in range(8):
            far = levels[np.abs(levels - a[p, g]) >= 10]
            a[p, g + 8] = far[np.random.randint(len(far))]
    return np.exp2(a.ravel()).repeat(32)


def f64(x):
    return np.asarray(x).astype(np.float64)


def striped(idx):
    return np.tile(idx.reshape(-1, 16).T, (8, 1)).astype(np.uint16)


def unstriped(offs):
    return offs[:16].T.reshape(-1).astype(np.int64)


def striped8(idx):
    return np.concatenate([x.reshape(-1, 16).T for x in idx]).astype(np.uint16)


def runs(offs, k):
    lists = np.stack([offs[16 * r : 16 * r + 16].T.reshape(-1) for r in range(8)]).astype(np.int64)
    return lists[np.arange(k) % 512 // 64]


def pack_weight(w):
    k, n = w.shape
    w = f64(np.asarray(w, np.float32).astype(ml_dtypes.bfloat16)).reshape(k // 32, 32, n)
    amax = np.abs(w).max(1)
    byte = np.clip(np.where(amax > 0, np.frexp(amax)[1] - 1 + 127 - 7, 1), 1, 254)
    scaled = (w * np.exp2(127.0 - byte)[:, None, :]).reshape(k, n).astype(np.float32)
    words = np.ascontiguousarray(scaled.reshape(k // 512, 128, 4, n).transpose(0, 1, 3, 2)).astype(ml_dtypes.float8_e4m3fn).view(np.uint8)
    return words, np.ascontiguousarray(byte.astype(np.uint8).reshape(k // 512, 16, n))


def unpack_weight(words, scales):
    g, p, n, _ = words.shape
    vals = np.ascontiguousarray(words).view(ml_dtypes.float8_e4m3fn).astype(np.float64) * np.repeat(np.exp2(scales.astype(np.float64) - 127.0), 8, axis=1)[..., None]
    return vals.transpose(0, 1, 3, 2).reshape(g * 512, n)


def sigmoid(v):
    return 1.0 / (1.0 + np.exp(-np.maximum(v, -700.0)))

def planes(y):
    n, m = y.shape
    v = y.astype(np.float32).astype(ml_dtypes.bfloat16).astype(np.float64).reshape(n // 32, 32, m)
    top = np.abs(v).max(1)
    byte = np.clip(np.where(top > 0, np.frexp(top)[1] - 1 + 127 - 7, 1), 1, 254)
    codes = (v * np.exp2(127.0 - byte)[:, None, :]).reshape(n, m).astype(np.float32).astype(ml_dtypes.float8_e4m3fn).view(np.uint8)
    words = codes.reshape(n // 512, 128, 4, m).transpose(0, 1, 3, 2)
    return np.ascontiguousarray(words), np.ascontiguousarray(byte.astype(np.uint8).reshape(n // 512, 16, m))


K, T, S, H, C, G, W = 512, 1024, 512, 512, 512, 2048, 256


def setup_inputs():
    n = np.random.standard_normal
    s = mx_kscale(K)[:, None]
    packed_xT = pack_weight(n((K, T)) * s)
    packed_w1 = pack_weight(n((K, H)) / np.sqrt(K) / s)
    packed_dT = pack_weight(n((K, G)) / s)
    return {
        "x_words": packed_xT[0],
        "x_scales": packed_xT[1],
        "w1_words": packed_w1[0],
        "w1_scales": packed_w1[1],
        "sl": np.random.uniform(1.0, 2.0, (H, 1)).astype(np.float32),
        "th": (0.5 * n((H, 1))).astype(np.float32),
        "gs": (np.random.uniform(0.5, 1.5, (K, 1)) / s).astype(np.float32),
        "gk": (np.random.uniform(0.5, 1.5, (K, 1)) * s).astype(np.float32),
        "d_words": packed_dT[0],
        "d_scales": packed_dT[1],
        "offs": striped(np.random.permutation(T)[:S]),
        "n1": striped8(np.stack([np.random.permutation(S) for _ in range(8)])),
        "n2": striped8(np.stack([np.random.permutation(S) for _ in range(8)])),
        "n3": striped(np.random.permutation(S)),
        "n4": striped(np.random.permutation(S)),
        "n5": striped(np.random.permutation(S)),
        "n6": striped(np.random.permutation(S)),
        "cand": striped(np.random.permutation(T)[:C]),
        "k1": striped8(np.random.randint(0, G, (8, H))),
        "n7": striped(np.random.permutation(S)[:W]),
        "n8": striped(np.random.permutation(S)[:W]),
    }


def reference(x_words, x_scales, w1_words, w1_scales, sl, th, gs, gk, d_words, d_scales, offs, n1, n2, n3, n4, n5, n6, cand, k1, n7, n8):
    d_k1 = unpack_weight(d_words, d_scales)[np.arange(K)[:, None], runs(k1, K)]
    xq = unpack_weight(x_words, x_scales)[:, unstriped(offs)]
    y = unpack_weight(w1_words, w1_scales).T @ xq
    z2 = f64(gk) * (0.75 * (y[:, unstriped(n3)] * y[:, unstriped(n4)] - (y[:, unstriped(n5)] * y[:, unstriped(n6)])))
    b = 0.0625 * ((d_k1.T @ mxq(z2, 0, "e4m3")))
    x_cand = unpack_weight(x_words, x_scales)[:, unstriped(cand)]
    sg = sigmoid(f64(sl) * (y[np.arange(H)[:, None], runs(n1, H)] - f64(th)))
    st = y * sg
    z = f64(gs) * (st - (0.5 * (st[np.arange(H)[:, None], runs(n2, H)])))
    a = 0.0625 * ((x_cand.T @ mxq(z, 0, "e4m3")))
    ra = b[:, unstriped(n8)] - (0.5 * a[:, unstriped(n7)])
    out = a.copy()
    out[:, unstriped(n7)] = ra
    return (out,) + planes(out)

@@ -1,0 +1,250 @@
+from contextlib import ExitStack
+
+import concourse.mybir as mybir
+
+F32 = mybir.dt.float32
+BF16 = mybir.dt.bfloat16
+I32 = mybir.dt.int32
+U32 = mybir.dt.uint32
+U16 = mybir.dt.uint16
+U8 = mybir.dt.uint8
+FP8X4 = mybir.dt.float8_e4m3fn_x4
+MULT = mybir.AluOpType.mult
+ADD = mybir.AluOpType.add
+SUB = mybir.AluOpType.subtract
+COPY = mybir.ActivationFunctionType.Copy
+SIGMOID = mybir.ActivationFunctionType.Sigmoid
+
+P = 128
+PACK = 4
+S = 512
+T = 1024
+G = 2048
+W = 256
+HALF = S // 2
+FLOPS = 3 * 2 * 512 * 512 * 512
+
+
+def tile_picked_cdkeyputbehpdet_none_po_kernel(
+    tc, x_words, x_scales, w1_words, w1_scales, sl, th, gs, gk, d_words, d_scales,
+    offs, n1, n2, n3, n4, n5, n6, cand, k1, n7, n8, out_0, out_1, out_2,
+):
+    nc = tc.nc
+    with ExitStack() as ctx:
+        keep = ctx.enter_context(tc.tile_pool(name="keep", bufs=1))
+        psum = ctx.enter_context(tc.psum_pool(name="psum", bufs=1))
+
+        def sb(name, shape, dtype):
+            return keep.tile(shape, dtype, name=name, align_bytes=64)
+
+        def load_list(name, src):
+            t = keep.tile(list(src.shape), U16, name=name)
+            nc.sync.dma_start(t[:], src)
+            return t
+
+        def words_of(src):
+            return src[0].rearrange("p n r -> p (n r)").bitcast(I32)
+
+        def dealt(ap):
+            return ap.rearrange("p (t m) -> p m t", t=PACK)
+
+        def as_read(ap):
+            return ap.rearrange("p (m t) -> p m t", t=PACK)
+
+        def load_scale_rows(dst, src):
+            for q in range(4):
+                nc.sync.dma_start(dst[32 * q : 32 * q + 4, :].bitcast(I32), src[0, 4 * q : 4 * q + 4, :].bitcast(I32))
+
+        def load_column(name, src):
+            t = sb(name, [P, PACK], F32)
+            nc.sync.dma_start(t[:], src.rearrange("(p t) o -> p (t o)", t=PACK))
+            return t
+
+        def bank(b, name):
+            return psum.tile([P, S], F32, name=name, tag="bank%d" % b)
+
+        xs = sb("xs", [P, T], U8)
+        w1s_raw = sb("w1s_raw", [P, S], U8)
+        ds = sb("ds", [P, G], U8)
+        ks = sb("ks", [P, S], U8)
+        nc.vector.memset(xs[:].bitcast(I32), 0)
+        nc.vector.memset(w1s_raw[:].bitcast(I32), 0)
+        nc.gpsimd.memset(ds[:].bitcast(I32), 0)
+        nc.gpsimd.memset(ks[:].bitcast(I32), 0)
+
+        xw = sb("xw", [P, T], I32)
+        w1w_raw = sb("w1w_raw", [P, S], I32)
+        l_offs = load_list("l_offs", offs)
+        nc.sync.dma_start(xw[:], words_of(x_words))
+        load_scale_rows(xs, x_scales)
+        nc.sync.dma_start(w1w_raw[:], words_of(w1_words))
+        load_scale_rows(w1s_raw, w1_scales)
+        c_sl = load_column("c_sl", sl)
+        c_th = load_column("c_th", th)
+        l_n1 = load_list("l_n1", n1)
+        l_cand = load_list("l_cand", cand)
+        c_gs = load_column("c_gs", gs)
+        l_k1 = load_list("l_k1", k1)
+        dw = sb("dw", [P, G], I32)
+        for e in range(2):
+            nc.sync.dma_start(ds[e:P:16, :].bitcast(I32), d_scales[0, e:16:2, :].bitcast(I32))
+        nc.sync.dma_start(dw[:], words_of(d_words))
+        c_gk = load_column("c_gk", gk)
+        l_n2 = load_list("l_n2", n2)
+        l_n3 = load_list("l_n3", n3)
+        l_n5 = load_list("l_n5", n5)
+        l_n4 = load_list("l_n4", n4)
+        l_n6 = load_list("l_n6", n6)
+        l_n7 = load_list("l_n7", n7)
+        l_n8 = load_list("l_n8", n8)
+
+        xq_s = sb("xq_s", [P, S], U8)
+        xq_w = sb("xq_w", [P, S], U32)
+        nc.vector.tensor_copy(xq_s[:], xs[:].indirect(l_offs[:]))
+        nc.vector.tensor_copy(xq_w[:], xw[:].bitcast(U32).indirect(l_offs[:]))
+        w1w = sb("w1w", [P, S], U32)
+        w1s = sb("w1s", [P, S], U8)
+        nc.scalar.copy(dealt(w1w[:]), as_read(w1w_raw[:].bitcast(U32)))
+        nc.vector.tensor_copy(dealt(w1s[:]), as_read(w1s_raw[:]))
+        c_nb = sb("c_nb", [P, PACK], F32)
+        nc.vector.scalar_tensor_tensor(c_nb[:], c_th[:], -1.0, c_sl[:], MULT, MULT)
+
+        def product(dst, lw, ls, t, rw, rs, cols):
+            rows = slice(P * t, P * (t + 1))
+            nc.tensor.matmul_mx(out=dst[:, cols], lhsT=lw[:, rows].bitcast(FP8X4), lhsT_scale=ls[:, rows],
+                                rhs=rw[:, cols].bitcast(FP8X4), rhs_scale=rs[:, cols], start=True, stop=True)
+
+        y_ps = [bank(t, "y_ps%d" % t) for t in range(PACK)]
+        for t in range(PACK):
+            product(y_ps[t], w1w, w1s, t, xq_w, xq_s, slice(0, S))
+
+        y = [sb("y%d" % t, [P, 2 * S], F32) for t in range(PACK)]
+        ys = [sb("ys%d" % t, [P, 2 * S], F32) for t in range(PACK)]
+        st = [sb("st%d" % t, [P, 2 * S], F32) for t in range(PACK)]
+        st_all = sb("st_all", [P, PACK, S], F32)
+        st2 = sb("st_n2", [P, PACK, S], F32)
+        for t in range(PACK):
+            if t < 2:
+                nc.scalar.copy(y[t][:, 0:S], y_ps[t][:])
+            else:
+                nc.vector.tensor_copy(y[t][:, 0:S], y_ps[t][:])
+        cw = sb("cw", [P, S], U32)
+        cs = sb("cs", [P, S], U8)
+        kw_g = sb("kw_g", [P, S], U32)
+        ks_g = sb("ks_g", [P, S], U8)
+        kw = sb("kw", [P, S], U32)
+        ks_d = sb("ks_d", [P, S], U8)
+
+        def packed_step(t):
+            if t == 0:
+                nc.vector.tensor_copy(dealt(cw[:]), xw[:].bitcast(U32).indirect(l_cand[:]))
+            elif t == 1:
+                nc.vector.tensor_copy(dealt(cs[:]), xs[:].indirect(l_cand[:]))
+            elif t == 2:
+                nc.vector.tensor_copy(ks_g[:], ds[:].indirect(l_k1[:]))
+                nc.vector.tensor_copy(dealt(ks_d[:]), as_read(ks_g[:]))
+                for j, src in enumerate((0, 1, 16, 17)):
+                    nc.sync.dma_start(ks[j:P:32, :].bitcast(I32), ks_d[src:P:32, :].bitcast(I32))
+            else:
+                nc.vector.tensor_copy(kw_g[:], dw[:].bitcast(U32).indirect(l_k1[:]))
+                nc.vector.tensor_copy(dealt(kw[:]), as_read(kw_g[:]))
+
+        for t in range(PACK):
+            col = slice(t, t + 1)
+            nc.scalar.activation(st[t][:, S : 2 * S], y[t][:].indirect(l_n1[:]), SIGMOID, bias=c_nb[:, col], scale=c_sl[:, col])
+            packed_step(t)
+            nc.vector.scalar_tensor_tensor(st[t][:, 0:S], y[t][:, 0:S], c_gs[:, col], st[t][:, S : 2 * S], MULT, MULT)
+            nc.sync.dma_start(st_all[:, t, :], st[t][:, 0:S])
+            nc.vector.tensor_scalar(ys[t][:, 0:S], y[t][:, 0:S], c_gk[:, col], 0.75, MULT, MULT)
+        for t in range(PACK):
+            nc.scalar.activation(st2[:, t, :], st[t][:].indirect(l_n2[:]), COPY, scale=0.5)
+
+        def woven_src(ap):
+            return ap.rearrange("p t (c i) -> p c t i", i=4)
+
+        def woven_dst(ap):
+            return ap.rearrange("p (c i) t -> p c t i", i=4)
+
+        def quantise(words, scales, src, cols):
+            nc.vector.quantize_mx(out=words[:, cols].bitcast(FP8X4), scales=scales[:, cols],
+                                  in_=src[:, cols, :].rearrange("p c t -> p (c t)"))
+
+        halves = [slice(0, HALF), slice(HALF, S)]
+        z_bf = sb("z_bf", [P, S, PACK], BF16)
+        z_w = sb("z_w", [P, S], U32)
+        z_s = sb("z_s", [P, S], U8)
+        nc.vector.tensor_tensor(woven_dst(z_bf[:]), woven_src(st_all[:]), woven_src(st2[:]), SUB)
+
+        g3 = sb("g3", [P, PACK, S], F32)
+        g5 = sb("g5", [P, PACK, S], F32)
+        pp, qq = st_all, st2
+        a_ps = [bank(PACK + t, "a_ps%d" % t) for t in range(PACK)]
+        for t in range(PACK):
+            nc.scalar.activation(g3[:, t, :], ys[t][:].indirect(l_n3[:]), COPY)
+            nc.scalar.activation(g5[:, t, :], ys[t][:].indirect(l_n5[:]), COPY)
+            nc.vector.tensor_tensor(pp[:, t, :], y[t][:].indirect(l_n4[:]), g3[:, t, :], MULT)
+            if t == 0:
+                quantise(z_w, z_s, z_bf, slice(0, S))
+                for u in range(PACK):
+                    product(a_ps[u], cw, cs, u, z_w, z_s, slice(0, S))
+            nc.vector.tensor_tensor(qq[:, t, :], y[t][:].indirect(l_n6[:]), g5[:, t, :], MULT)
+
+        res = [sb("res%d" % t, [P, S], F32) for t in range(PACK)]
+        g7 = [sb("g7_%d" % t, [P, W], F32) for t in range(PACK)]
+        for t in range(PACK):
+            nc.scalar.activation(res[t][:], a_ps[t][:], COPY, scale=0.0625)
+            nc.scalar.activation(g7[t][:], res[t][:].indirect(l_n7[:]), COPY, scale=-0.5)
+
+        z2_bf = sb("z2_bf", [P, S, PACK], BF16)
+        z2_w = sb("z2_w", [P, S], U32)
+        z2_s = sb("z2_s", [P, S], U8)
+        b_ps = [[bank(2 * h + u, "b_ps%d%d" % (h, u)) for u in range(2)] for h in range(2)]
+        b = [sb("b%d" % t, [P, S], F32) for t in range(PACK)]
+        for cols in halves:
+            nc.vector.tensor_tensor(woven_dst(z2_bf[:, cols, :]), woven_src(pp[:, :, cols]), woven_src(qq[:, :, cols]), SUB)
+        for h, cols in enumerate(halves):
+            quantise(z2_w, z2_s, z2_bf, cols)
+            for t in range(PACK):
+                rows = slice(P * t, P * (t + 1))
+                dst = b_ps[h][t % 2][:, HALF * (t // 2) : HALF * (t // 2 + 1)]
+                nc.tensor.matmul_mx(out=dst, lhsT=kw[:, rows].bitcast(FP8X4), lhsT_scale=ks[:, rows],
+                                    rhs=z2_w[:, cols].bitcast(FP8X4), rhs_scale=z2_s[:, cols], start=True, stop=True)
+            for t in range(PACK):
+                src = b_ps[h][t % 2][:, HALF * (t // 2) : HALF * (t // 2 + 1)]
+                if h == 1 and t % 2 == 1:
+                    nc.vector.tensor_scalar(b[t][:, cols], src, 0.0625, None, MULT)
+                else:
+                    nc.scalar.activation(b[t][:, cols], src, COPY, scale=0.0625)
+
+        g8 = [sb("g8_%d" % t, [P, W], F32) for t in range(PACK)]
+        stage = sb("stage", [P, PACK, S], F32)
+        out_rows = out_0.rearrange("(p t) n -> p t n", t=PACK)
+        for t in range(PACK):
+            if t % 2 == 0:
+                nc.scalar.activation(g8[t][:], b[t][:].indirect(l_n8[:]), COPY)
+            else:
+                nc.vector.tensor_tensor(g8[t][:], b[t][:].indirect(l_n8[:]), g7[t][:], ADD)
+        for t in range(PACK):
+            if t % 2 == 0:
+                nc.vector.tensor_tensor(res[t][:].indirect(l_n7[:]), g8[t][:], g7[t][:], ADD)
+            else:
+                nc.scalar.activation(res[t][:].indirect(l_n7[:]), g8[t][:], COPY)
+            nc.sync.dma_start(out_rows[:, t, :], res[t][:])
+        for t in range(PACK):
+            if t == 1:
+                nc.scalar.copy(stage[:, t, :], res[t][:])
+            else:
+                nc.vector.tensor_copy(stage[:, t, :], res[t][:])
+
+        o_bf = sb("o_bf", [P, S, PACK], BF16)
+        o_w = sb("o_w", [P, S], U32)
+        o_s = sb("o_s", [P, S], U8)
+        out_words = words_of(out_1)
+        for eng_copy, cols in ((nc.vector.tensor_copy, slice(0, 320)), (nc.scalar.copy, slice(320, S))):
+            eng_copy(woven_dst(o_bf[:, cols, :]), woven_src(stage[:, :, cols]))
+        for cols in halves:
+            quantise(o_w, o_s, o_bf, cols)
+            nc.sync.dma_start(out_words[:, cols], o_w[:, cols].bitcast(I32))
+        for q in range(4):
+            eng = nc.sync if q % 2 == 0 else nc.scalar
+            eng.dma_start(out_2[0, 4 * q : 4 * q + 4, :].bitcast(I32), o_s[32 * q : 32 * q + 4, :].bitcast(I32))

@@ -34,8 +34,8 @@ def tile_picked_cdkeyputbehpdet_none_po_kernel(
         keep = ctx.enter_context(tc.tile_pool(name="keep", bufs=1))
         psum = ctx.enter_context(tc.psum_pool(name="psum", bufs=1))
 
-        def sb(name, shape, dtype):
-            return keep.tile(shape, dtype, name=name, align_bytes=64)
+        def sb(name, shape, dtype, tag=""):
+            return keep.tile(shape, dtype, name=name, tag=tag or name, align_bytes=64)
 
         def load_list(name, src):
             t = keep.tile(list(src.shape), U16, name=name)
@@ -55,9 +55,9 @@ def tile_picked_cdkeyputbehpdet_none_po_kernel(
             for q in range(4):
                 nc.sync.dma_start(dst[32 * q : 32 * q + 4, :].bitcast(I32), src[0, 4 * q : 4 * q + 4, :].bitcast(I32))
 
-        def load_column(name, src):
+        def load_column(name, src, eng):
             t = sb(name, [P, PACK], F32)
-            nc.sync.dma_start(t[:], src.rearrange("(p t) o -> p (t o)", t=PACK))
+            eng.dma_start(t[:], src.rearrange("(p t) o -> p (t o)", t=PACK))
             return t
 
         def bank(b, name):
@@ -67,29 +67,29 @@ def tile_picked_cdkeyputbehpdet_none_po_kernel(
         w1s_raw = sb("w1s_raw", [P, S], U8)
         ds = sb("ds", [P, G], U8)
         ks = sb("ks", [P, S], U8)
-        nc.vector.memset(xs[:].bitcast(I32), 0)
+        nc.gpsimd.memset(xs[:].bitcast(I32), 0)
         nc.vector.memset(w1s_raw[:].bitcast(I32), 0)
-        nc.gpsimd.memset(ds[:].bitcast(I32), 0)
-        nc.gpsimd.memset(ks[:].bitcast(I32), 0)
+        nc.vector.memset(ds[:].bitcast(I32), 0)
+        nc.vector.memset(ks[:].bitcast(I32), 0)
 
         xw = sb("xw", [P, T], I32)
         w1w_raw = sb("w1w_raw", [P, S], I32)
         l_offs = load_list("l_offs", offs)
-        nc.sync.dma_start(xw[:], words_of(x_words))
-        load_scale_rows(xs, x_scales)
         nc.sync.dma_start(w1w_raw[:], words_of(w1_words))
+        load_scale_rows(xs, x_scales)
+        nc.sync.dma_start(xw[:], words_of(x_words))
         load_scale_rows(w1s_raw, w1_scales)
-        c_sl = load_column("c_sl", sl)
-        c_th = load_column("c_th", th)
-        l_n1 = load_list("l_n1", n1)
         l_cand = load_list("l_cand", cand)
-        c_gs = load_column("c_gs", gs)
+        c_sl = load_column("c_sl", sl, nc.sync)
+        c_th = load_column("c_th", th, nc.sync)
+        l_n1 = load_list("l_n1", n1)
+        c_gs = load_column("c_gs", gs, nc.gpsimd)
+        c_gk = load_column("c_gk", gk, nc.gpsimd)
         l_k1 = load_list("l_k1", k1)
         dw = sb("dw", [P, G], I32)
         for e in range(2):
             nc.sync.dma_start(ds[e:P:16, :].bitcast(I32), d_scales[0, e:16:2, :].bitcast(I32))
         nc.sync.dma_start(dw[:], words_of(d_words))
-        c_gk = load_column("c_gk", gk)
         l_n2 = load_list("l_n2", n2)
         l_n3 = load_list("l_n3", n3)
         l_n5 = load_list("l_n5", n5)
@@ -101,13 +101,18 @@ def tile_picked_cdkeyputbehpdet_none_po_kernel(
         xq_s = sb("xq_s", [P, S], U8)
         xq_w = sb("xq_w", [P, S], U32)
         nc.vector.tensor_copy(xq_s[:], xs[:].indirect(l_offs[:]))
-        nc.vector.tensor_copy(xq_w[:], xw[:].bitcast(U32).indirect(l_offs[:]))
-        w1w = sb("w1w", [P, S], U32)
         w1s = sb("w1s", [P, S], U8)
-        nc.scalar.copy(dealt(w1w[:]), as_read(w1w_raw[:].bitcast(U32)))
         nc.vector.tensor_copy(dealt(w1s[:]), as_read(w1s_raw[:]))
+        halves = [slice(0, HALF), slice(HALF, S)]
+        for h, cols in enumerate(halves):
+            nc.vector.tensor_copy(xq_w[:, cols], xw[:].bitcast(U32).indirect(l_offs[:, 16 * h : 16 * (h + 1)]))
+        w1w = sb("w1w", [P, S], U32)
+        nc.scalar.copy(dealt(w1w[:]), as_read(w1w_raw[:].bitcast(U32)))
         c_nb = sb("c_nb", [P, PACK], F32)
-        nc.vector.scalar_tensor_tensor(c_nb[:], c_th[:], -1.0, c_sl[:], MULT, MULT)
+        c_nth = sb("c_nth", [P, PACK], F32)
+        nc.scalar.activation(c_nth[:], c_th[:], COPY, scale=-1.0)
+        for t in range(PACK):
+            nc.scalar.activation(c_nb[:, t : t + 1], c_nth[:, t : t + 1], COPY, scale=c_sl[:, t : t + 1])
 
         def product(dst, lw, ls, t, rw, rs, cols):
             rows = slice(P * t, P * (t + 1))
@@ -115,49 +120,54 @@ def tile_picked_cdkeyputbehpdet_none_po_kernel(
                                 rhs=rw[:, cols].bitcast(FP8X4), rhs_scale=rs[:, cols], start=True, stop=True)
 
         y_ps = [bank(t, "y_ps%d" % t) for t in range(PACK)]
-        for t in range(PACK):
-            product(y_ps[t], w1w, w1s, t, xq_w, xq_s, slice(0, S))
-
         y = [sb("y%d" % t, [P, 2 * S], F32) for t in range(PACK)]
         ys = [sb("ys%d" % t, [P, 2 * S], F32) for t in range(PACK)]
-        st = [sb("st%d" % t, [P, 2 * S], F32) for t in range(PACK)]
-        st_all = sb("st_all", [P, PACK, S], F32)
-        st2 = sb("st_n2", [P, PACK, S], F32)
-        for t in range(PACK):
+        sg = [sb("sg%d" % t, [P, S], F32) for t in range(PACK)]
+        for cols, dst in zip(halves, (y_ps[0], bank(PACK, "y_ps0_right"))):
+            product(dst, w1w, w1s, 0, xq_w, xq_s, cols)
+            nc.scalar.copy(y[0][:, cols], dst[:, cols])
+        for t in range(1, PACK):
+            product(y_ps[t], w1w, w1s, t, xq_w, xq_s, slice(0, S))
             if t < 2:
                 nc.scalar.copy(y[t][:, 0:S], y_ps[t][:])
             else:
                 nc.vector.tensor_copy(y[t][:, 0:S], y_ps[t][:])
+        for t in range(PACK):
+            nc.gpsimd.tensor_scalar(ys[t][:, 0:S], y[t][:, 0:S], c_gk[:, t : t + 1], 0.75, MULT, MULT)
+
+        st_all = sb("st_all", [P, PACK, S], F32)
+        st2 = sb("st_n2", [P, PACK, S], F32)
         cw = sb("cw", [P, S], U32)
         cs = sb("cs", [P, S], U8)
-        kw_g = sb("kw_g", [P, S], U32)
-        ks_g = sb("ks_g", [P, S], U8)
         kw = sb("kw", [P, S], U32)
         ks_d = sb("ks_d", [P, S], U8)
-
-        def packed_step(t):
+        nc.vector.tensor_copy(dealt(cw[:]), xw[:].bitcast(U32).indirect(l_cand[:]))
+        nc.vector.tensor_copy(dealt(cs[:]), xs[:].indirect(l_cand[:]))
+        st = []
+        for t in range(PACK):
+            col = slice(t, t + 1)
+            nc.scalar.activation(sg[t][:], y[t][:].indirect(l_n1[:]), SIGMOID, bias=c_nb[:, col], scale=c_sl[:, col])
             if t == 0:
-                nc.vector.tensor_copy(dealt(cw[:]), xw[:].bitcast(U32).indirect(l_cand[:]))
-            elif t == 1:
-                nc.vector.tensor_copy(dealt(cs[:]), xs[:].indirect(l_cand[:]))
-            elif t == 2:
+                ks_g = sb("ks_g", [P, S], U8, tag="st0")
                 nc.vector.tensor_copy(ks_g[:], ds[:].indirect(l_k1[:]))
                 nc.vector.tensor_copy(dealt(ks_d[:]), as_read(ks_g[:]))
                 for j, src in enumerate((0, 1, 16, 17)):
-                    nc.sync.dma_start(ks[j:P:32, :].bitcast(I32), ks_d[src:P:32, :].bitcast(I32))
-            else:
+                    nc.gpsimd.dma_start(ks[j:P:32, :].bitcast(I32), ks_d[src:P:32, :].bitcast(I32))
+            if t == 3:
+                kw_g = sb("kw_g", [P, S], U32, tag="st3")
                 nc.vector.tensor_copy(kw_g[:], dw[:].bitcast(U32).indirect(l_k1[:]))
                 nc.vector.tensor_copy(dealt(kw[:]), as_read(kw_g[:]))
-
+            st.append(sb("st%d" % t, [P, (2 if t < 2 else 4) * S], F32))
+            nc.vector.scalar_tensor_tensor(st[t][:, 0:S], y_ps[t][:] if t else y[t][:, 0:S], c_gs[:, col], sg[t][:], MULT, MULT)
+            if t < PACK - 1:
+                nc.sync.dma_start(st_all[:, t, :], st[t][:, 0:S])
+            else:
+                nc.vector.tensor_copy(st_all[:, t, :], st[t][:, 0:S])
         for t in range(PACK):
-            col = slice(t, t + 1)
-            nc.scalar.activation(st[t][:, S : 2 * S], y[t][:].indirect(l_n1[:]), SIGMOID, bias=c_nb[:, col], scale=c_sl[:, col])
-            packed_step(t)
-            nc.vector.scalar_tensor_tensor(st[t][:, 0:S], y[t][:, 0:S], c_gs[:, col], st[t][:, S : 2 * S], MULT, MULT)
-            nc.sync.dma_start(st_all[:, t, :], st[t][:, 0:S])
-            nc.vector.tensor_scalar(ys[t][:, 0:S], y[t][:, 0:S], c_gk[:, col], 0.75, MULT, MULT)
-        for t in range(PACK):
-            nc.scalar.activation(st2[:, t, :], st[t][:].indirect(l_n2[:]), COPY, scale=0.5)
+            if t < PACK - 1:
+                nc.scalar.activation(st2[:, t, :], st[t][:].indirect(l_n2[:]), COPY, scale=0.5)
+            else:
+                nc.vector.tensor_scalar(st2[:, t, :], st[t][:].indirect(l_n2[:]), 0.5, 0.0, MULT, ADD)
 
         def woven_src(ap):
             return ap.rearrange("p t (c i) -> p c t i", i=4)
@@ -169,25 +179,24 @@ def tile_picked_cdkeyputbehpdet_none_po_kernel(
             nc.vector.quantize_mx(out=words[:, cols].bitcast(FP8X4), scales=scales[:, cols],
                                   in_=src[:, cols, :].rearrange("p c t -> p (c t)"))
 
-        halves = [slice(0, HALF), slice(HALF, S)]
         z_bf = sb("z_bf", [P, S, PACK], BF16)
         z_w = sb("z_w", [P, S], U32)
         z_s = sb("z_s", [P, S], U8)
         nc.vector.tensor_tensor(woven_dst(z_bf[:]), woven_src(st_all[:]), woven_src(st2[:]), SUB)
 
-        g3 = sb("g3", [P, PACK, S], F32)
-        g5 = sb("g5", [P, PACK, S], F32)
+        spare = [st[u][:, S * j : S * (j + 1)] for u in (2, 3) for j in (1, 2, 3)] + [st[u][:, 0:S] for u in (2, 3)]
+        g3, g5 = spare[0::2], spare[1::2]
         pp, qq = st_all, st2
         a_ps = [bank(PACK + t, "a_ps%d" % t) for t in range(PACK)]
         for t in range(PACK):
-            nc.scalar.activation(g3[:, t, :], ys[t][:].indirect(l_n3[:]), COPY)
-            nc.scalar.activation(g5[:, t, :], ys[t][:].indirect(l_n5[:]), COPY)
-            nc.vector.tensor_tensor(pp[:, t, :], y[t][:].indirect(l_n4[:]), g3[:, t, :], MULT)
+            nc.scalar.activation(g3[t], ys[t][:].indirect(l_n3[:]), COPY)
+            nc.scalar.activation(g5[t], ys[t][:].indirect(l_n5[:]), COPY)
+            nc.vector.tensor_tensor(pp[:, t, :], y[t][:].indirect(l_n4[:]), g3[t], MULT)
             if t == 0:
                 quantise(z_w, z_s, z_bf, slice(0, S))
                 for u in range(PACK):
                     product(a_ps[u], cw, cs, u, z_w, z_s, slice(0, S))
-            nc.vector.tensor_tensor(qq[:, t, :], y[t][:].indirect(l_n6[:]), g5[:, t, :], MULT)
+            nc.vector.tensor_tensor(qq[:, t, :], y[t][:].indirect(l_n6[:]), g5[t], MULT)
 
         res = [sb("res%d" % t, [P, S], F32) for t in range(PACK)]
         g7 = [sb("g7_%d" % t, [P, W], F32) for t in range(PACK)]

@@ -83,12 +83,12 @@ def tile_picked_cdkeyputbehpdet_none_po_kernel(
         c_sl = load_column("c_sl", sl, nc.sync)
         c_th = load_column("c_th", th, nc.sync)
         l_n1 = load_list("l_n1", n1)
-        c_gs = load_column("c_gs", gs, nc.gpsimd)
-        c_gk = load_column("c_gk", gk, nc.gpsimd)
         l_k1 = load_list("l_k1", k1)
         dw = sb("dw", [P, G], I32)
         for e in range(2):
             nc.sync.dma_start(ds[e:P:16, :].bitcast(I32), d_scales[0, e:16:2, :].bitcast(I32))
+        c_gs = load_column("c_gs", gs, nc.sync)
+        c_gk = load_column("c_gk", gk, nc.sync)
         nc.sync.dma_start(dw[:], words_of(d_words))
         l_n2 = load_list("l_n2", n2)
         l_n3 = load_list("l_n3", n3)
@@ -114,6 +114,9 @@ def tile_picked_cdkeyputbehpdet_none_po_kernel(
         for t in range(PACK):
             nc.scalar.activation(c_nb[:, t : t + 1], c_nth[:, t : t + 1], COPY, scale=c_sl[:, t : t + 1])
 
+        c_gk75 = sb("c_gk75", [P, PACK], F32)
+        nc.vector.tensor_scalar(c_gk75[:], c_gk[:], 0.75, None, MULT)
+
         def product(dst, lw, ls, t, rw, rs, cols):
             rows = slice(P * t, P * (t + 1))
             nc.tensor.matmul_mx(out=dst[:, cols], lhsT=lw[:, rows].bitcast(FP8X4), lhsT_scale=ls[:, rows],
@@ -121,7 +124,7 @@ def tile_picked_cdkeyputbehpdet_none_po_kernel(
 
         y_ps = [bank(t, "y_ps%d" % t) for t in range(PACK)]
         y = [sb("y%d" % t, [P, 2 * S], F32) for t in range(PACK)]
-        ys = [sb("ys%d" % t, [P, 2 * S], F32) for t in range(PACK)]
+        ys = [sb("ys%d" % t, [P, 2 * S], F32)[:] for t in range(2)]
         sg = [sb("sg%d" % t, [P, S], F32) for t in range(PACK)]
         for cols, dst in zip(halves, (y_ps[0], bank(PACK, "y_ps0_right"))):
             product(dst, w1w, w1s, 0, xq_w, xq_s, cols)
@@ -132,8 +135,6 @@ def tile_picked_cdkeyputbehpdet_none_po_kernel(
                 nc.scalar.copy(y[t][:, 0:S], y_ps[t][:])
             else:
                 nc.vector.tensor_copy(y[t][:, 0:S], y_ps[t][:])
-        for t in range(PACK):
-            nc.gpsimd.tensor_scalar(ys[t][:, 0:S], y[t][:, 0:S], c_gk[:, t : t + 1], 0.75, MULT, MULT)
 
         st_all = sb("st_all", [P, PACK, S], F32)
         st2 = sb("st_n2", [P, PACK, S], F32)
@@ -147,27 +148,32 @@ def tile_picked_cdkeyputbehpdet_none_po_kernel(
         for t in range(PACK):
             col = slice(t, t + 1)
             nc.scalar.activation(sg[t][:], y[t][:].indirect(l_n1[:]), SIGMOID, bias=c_nb[:, col], scale=c_sl[:, col])
-            if t == 0:
-                ks_g = sb("ks_g", [P, S], U8, tag="st0")
-                nc.vector.tensor_copy(ks_g[:], ds[:].indirect(l_k1[:]))
-                nc.vector.tensor_copy(dealt(ks_d[:]), as_read(ks_g[:]))
+            h = t % 2
+            part = l_k1[:, 16 * h : 16 * (h + 1)]
+            places = slice(64 * h, 64 * (h + 1))
+            if t < 2:
+                picked = sb("ks_g%d" % h, [P, HALF], U8, tag="st%d" % t)
+                nc.vector.tensor_copy(picked[:], ds[:].indirect(part))
+                nc.vector.tensor_copy(dealt(ks_d[:])[:, places, :], as_read(picked[:]))
+            else:
+                picked = sb("kw_g%d" % h, [P, HALF], U32, tag="st%d" % t)
+                nc.vector.tensor_copy(picked[:], dw[:].bitcast(U32).indirect(part))
+                nc.vector.tensor_copy(dealt(kw[:])[:, places, :], as_read(picked[:]))
+            if t == 1:
                 for j, src in enumerate((0, 1, 16, 17)):
-                    nc.gpsimd.dma_start(ks[j:P:32, :].bitcast(I32), ks_d[src:P:32, :].bitcast(I32))
-            if t == 3:
-                kw_g = sb("kw_g", [P, S], U32, tag="st3")
-                nc.vector.tensor_copy(kw_g[:], dw[:].bitcast(U32).indirect(l_k1[:]))
-                nc.vector.tensor_copy(dealt(kw[:]), as_read(kw_g[:]))
-            st.append(sb("st%d" % t, [P, (2 if t < 2 else 4) * S], F32))
+                    nc.sync.dma_start(ks[j:P:32, :].bitcast(I32), ks_d[src:P:32, :].bitcast(I32))
+            st.append(sb("st%d" % t, [P, (2 if t < 3 else 4) * S], F32))
             nc.vector.scalar_tensor_tensor(st[t][:, 0:S], y_ps[t][:] if t else y[t][:, 0:S], c_gs[:, col], sg[t][:], MULT, MULT)
             if t < PACK - 1:
                 nc.sync.dma_start(st_all[:, t, :], st[t][:, 0:S])
             else:
                 nc.vector.tensor_copy(st_all[:, t, :], st[t][:, 0:S])
+        for t in range(2):
+            nc.vector.tensor_scalar(ys[t][:, 0:S], y[t][:, 0:S], c_gk75[:, t : t + 1], None, MULT)
         for t in range(PACK):
-            if t < PACK - 1:
-                nc.scalar.activation(st2[:, t, :], st[t][:].indirect(l_n2[:]), COPY, scale=0.5)
-            else:
-                nc.vector.tensor_scalar(st2[:, t, :], st[t][:].indirect(l_n2[:]), 0.5, 0.0, MULT, ADD)
+            nc.scalar.activation(st2[:, t, :], st[t][:].indirect(l_n2[:]), COPY, scale=0.5)
+        ys_late = sb("ys_late", [P, 3 * S], F32, tag="sg3")
+        ys = ys + [ys_late[:, 0 : 2 * S], ys_late[:, S : 3 * S]]
 
         def woven_src(ap):
             return ap.rearrange("p t (c i) -> p c t i", i=4)
@@ -184,13 +190,15 @@ def tile_picked_cdkeyputbehpdet_none_po_kernel(
         z_s = sb("z_s", [P, S], U8)
         nc.vector.tensor_tensor(woven_dst(z_bf[:]), woven_src(st_all[:]), woven_src(st2[:]), SUB)
 
-        spare = [st[u][:, S * j : S * (j + 1)] for u in (2, 3) for j in (1, 2, 3)] + [st[u][:, 0:S] for u in (2, 3)]
+        spare = [st[3][:, S * j : S * (j + 1)] for j in (1, 2, 3, 0)] + [sb("g_%d" % j, [P, S], F32)[:] for j in range(4)]
         g3, g5 = spare[0::2], spare[1::2]
         pp, qq = st_all, st2
         a_ps = [bank(PACK + t, "a_ps%d" % t) for t in range(PACK)]
         for t in range(PACK):
-            nc.scalar.activation(g3[t], ys[t][:].indirect(l_n3[:]), COPY)
-            nc.scalar.activation(g5[t], ys[t][:].indirect(l_n5[:]), COPY)
+            if t >= 2:
+                nc.scalar.activation(ys[t][:, 0:S], y[t][:, 0:S], COPY, scale=c_gk75[:, t : t + 1])
+            nc.scalar.activation(g3[t], ys[t].indirect(l_n3[:]), COPY)
+            nc.scalar.activation(g5[t], ys[t].indirect(l_n5[:]), COPY)
             nc.vector.tensor_tensor(pp[:, t, :], y[t][:].indirect(l_n4[:]), g3[t], MULT)
             if t == 0:
                 quantise(z_w, z_s, z_bf, slice(0, S))
@@ -249,7 +257,7 @@ def tile_picked_cdkeyputbehpdet_none_po_kernel(
         o_w = sb("o_w", [P, S], U32)
         o_s = sb("o_s", [P, S], U8)
         out_words = words_of(out_1)
-        for eng_copy, cols in ((nc.vector.tensor_copy, slice(0, 320)), (nc.scalar.copy, slice(320, S))):
+        for eng_copy, cols in zip((nc.vector.tensor_copy, nc.scalar.copy), halves):
             eng_copy(woven_dst(o_bf[:, cols, :]), woven_src(stage[:, :, cols]))
         for cols in halves:
             quantise(o_w, o_s, o_bf, cols)

@@ -22,7 +22,10 @@ T = 1024
 G = 2048
 W = 256
 HALF = S // 2
-FLOPS = 3 * 2 * 512 * 512 * 512
+GROUP = 16
+QUADRANT = 32
+SCORE_SCALE = 0.0625
+FLOPS = 3 * 2 * S * S * S
 
 
 def tile_picked_cdkeyputbehpdet_none_po_kernel(
@@ -30,6 +33,7 @@ def tile_picked_cdkeyputbehpdet_none_po_kernel(
     offs, n1, n2, n3, n4, n5, n6, cand, k1, n7, n8, out_0, out_1, out_2,
 ):
     nc = tc.nc
+    halves = [slice(0, HALF), slice(HALF, S)]
     with ExitStack() as ctx:
         keep = ctx.enter_context(tc.tile_pool(name="keep", bufs=1))
         psum = ctx.enter_context(tc.psum_pool(name="psum", bufs=1))
@@ -37,59 +41,90 @@ def tile_picked_cdkeyputbehpdet_none_po_kernel(
         def sb(name, shape, dtype, tag=""):
             return keep.tile(shape, dtype, name=name, tag=tag or name, align_bytes=64)
 
-        def load_list(name, src):
-            t = keep.tile(list(src.shape), U16, name=name)
-            nc.sync.dma_start(t[:], src)
-            return t
+        def bank(number, name):
+            return psum.tile([P, S], F32, name=name, tag="bank%d" % number)
 
-        def words_of(src):
-            return src[0].rearrange("p n r -> p (n r)").bitcast(I32)
+        def load_list(name, src):
+            tile = keep.tile(list(src.shape), U16, name=name)
+            nc.sync.dma_start(tile[:], src)
+            return tile
+
+        def load_row_factors(name, src):
+            tile = sb(name, [P, PACK], F32)
+            nc.sync.dma_start(tile[:], src.rearrange("(p t) o -> p (t o)", t=PACK))
+            return tile
+
+        def load_scale_rows(dst, src):
+            for q in range(P // QUADRANT):
+                nc.sync.dma_start(dst[QUADRANT * q : QUADRANT * q + 4, :].bitcast(I32), src[0, 4 * q : 4 * q + 4, :].bitcast(I32))
+
+        def words_of(dram):
+            return dram[0].rearrange("p n r -> p (n r)").bitcast(I32)
 
         def dealt(ap):
             return ap.rearrange("p (t m) -> p m t", t=PACK)
 
-        def as_read(ap):
+        def plain(ap):
             return ap.rearrange("p (m t) -> p m t", t=PACK)
 
-        def load_scale_rows(dst, src):
-            for q in range(4):
-                nc.sync.dma_start(dst[32 * q : 32 * q + 4, :].bitcast(I32), src[0, 4 * q : 4 * q + 4, :].bitcast(I32))
+        def half_list(tile, h):
+            columns = HALF // GROUP
+            return tile[:, columns * h : columns * (h + 1)]
 
-        def load_column(name, src, eng):
-            t = sb(name, [P, PACK], F32)
-            eng.dma_start(t[:], src.rearrange("(p t) o -> p (t o)", t=PACK))
-            return t
+        def product(dst, words, scales, t, moving_words, moving_scales, cols):
+            rows = slice(P * t, P * (t + 1))
+            nc.tensor.matmul_mx(
+                out=dst, lhsT=words[:, rows].bitcast(FP8X4), lhsT_scale=scales[:, rows],
+                rhs=moving_words[:, cols].bitcast(FP8X4), rhs_scale=moving_scales[:, cols], start=True, stop=True,
+            )
 
-        def bank(b, name):
-            return psum.tile([P, S], F32, name=name, tag="bank%d" % b)
+        def from_tiles(ap, run):
+            return ap.rearrange("p t (c i) -> p c t i", i=run)
 
-        xs = sb("xs", [P, T], U8)
-        w1s_raw = sb("w1s_raw", [P, S], U8)
-        ds = sb("ds", [P, G], U8)
-        ks = sb("ks", [P, S], U8)
-        nc.gpsimd.memset(xs[:].bitcast(I32), 0)
-        nc.vector.memset(w1s_raw[:].bitcast(I32), 0)
-        nc.vector.memset(ds[:].bitcast(I32), 0)
-        nc.vector.memset(ks[:].bitcast(I32), 0)
+        def into_woven(ap, run):
+            return ap.rearrange("p (c i) t -> p c t i", i=run)
 
-        xw = sb("xw", [P, T], I32)
-        w1w_raw = sb("w1w_raw", [P, S], I32)
+        def weave_difference(dst, left, right, cols):
+            nc.vector.tensor_tensor(into_woven(dst[:, cols, :], 2), from_tiles(left[:, :, cols], 2), from_tiles(right[:, :, cols], 2), SUB)
+
+        def quantise(words, scales, woven, cols):
+            nc.vector.quantize_mx(
+                out=words[:, cols].bitcast(FP8X4), scales=scales[:, cols],
+                in_=woven[:, cols, :].rearrange("p c t -> p (c t)"),
+            )
+
+        warm_in = sb("warm_in", [P, 1], F32)
+        warm_out = sb("warm_out", [P, 1], F32)
+        nc.vector.memset(warm_in[:], 0.0)
+        nc.scalar.activation(warm_out[:], warm_in[:], SIGMOID)
+
+        x_s = sb("x_s", [P, T], U8)
+        w1_s_plain = sb("w1_s_plain", [P, S], U8)
+        d_s = sb("d_s", [P, G], U8)
+        key_s = sb("key_s", [P, S], U8)
+        nc.gpsimd.memset(x_s[:].bitcast(I32), 0)
+        nc.vector.memset(w1_s_plain[:].bitcast(I32), 0)
+        nc.vector.memset(d_s[:].bitcast(I32), 0)
+        nc.vector.memset(key_s[:].bitcast(I32), 0)
+
+        x_w = sb("x_w", [P, T], I32)
+        w1_w_plain = sb("w1_w_plain", [P, S], I32)
+        d_w = sb("d_w", [P, G], I32)
         l_offs = load_list("l_offs", offs)
-        nc.sync.dma_start(w1w_raw[:], words_of(w1_words))
-        load_scale_rows(xs, x_scales)
-        nc.sync.dma_start(xw[:], words_of(x_words))
-        load_scale_rows(w1s_raw, w1_scales)
+        nc.sync.dma_start(w1_w_plain[:], words_of(w1_words))
+        slope = load_row_factors("slope", sl)
+        threshold = load_row_factors("threshold", th)
+        load_scale_rows(x_s, x_scales)
+        nc.sync.dma_start(x_w[:], words_of(x_words))
+        load_scale_rows(w1_s_plain, w1_scales)
         l_cand = load_list("l_cand", cand)
-        c_sl = load_column("c_sl", sl, nc.sync)
-        c_th = load_column("c_th", th, nc.sync)
         l_n1 = load_list("l_n1", n1)
         l_k1 = load_list("l_k1", k1)
-        dw = sb("dw", [P, G], I32)
         for e in range(2):
-            nc.sync.dma_start(ds[e:P:16, :].bitcast(I32), d_scales[0, e:16:2, :].bitcast(I32))
-        c_gs = load_column("c_gs", gs, nc.sync)
-        c_gk = load_column("c_gk", gk, nc.sync)
-        nc.sync.dma_start(dw[:], words_of(d_words))
+            nc.sync.dma_start(d_s[e:P:GROUP, :].bitcast(I32), d_scales[0, e:16:2, :].bitcast(I32))
+        z_gain = load_row_factors("z_gain", gs)
+        key_gain = load_row_factors("key_gain", gk)
+        nc.sync.dma_start(d_w[:], words_of(d_words))
         l_n2 = load_list("l_n2", n2)
         l_n3 = load_list("l_n3", n3)
         l_n5 = load_list("l_n5", n5)
@@ -98,170 +133,141 @@ def tile_picked_cdkeyputbehpdet_none_po_kernel(
         l_n7 = load_list("l_n7", n7)
         l_n8 = load_list("l_n8", n8)
 
-        xq_s = sb("xq_s", [P, S], U8)
-        xq_w = sb("xq_w", [P, S], U32)
-        nc.vector.tensor_copy(xq_s[:], xs[:].indirect(l_offs[:]))
-        w1s = sb("w1s", [P, S], U8)
-        nc.vector.tensor_copy(dealt(w1s[:]), as_read(w1s_raw[:]))
-        halves = [slice(0, HALF), slice(HALF, S)]
+        picked_s = sb("picked_s", [P, S], U8)
+        picked_w = sb("picked_w", [P, S], U32)
+        w1_s = sb("w1_s", [P, S], U8)
+        w1_w = sb("w1_w", [P, S], U32)
+        nc.vector.tensor_copy(picked_s[:], x_s[:].indirect(l_offs[:]))
+        nc.vector.tensor_copy(dealt(w1_s[:]), plain(w1_s_plain[:]))
         for h, cols in enumerate(halves):
-            nc.vector.tensor_copy(xq_w[:, cols], xw[:].bitcast(U32).indirect(l_offs[:, 16 * h : 16 * (h + 1)]))
-        w1w = sb("w1w", [P, S], U32)
-        nc.scalar.copy(dealt(w1w[:]), as_read(w1w_raw[:].bitcast(U32)))
-        c_nb = sb("c_nb", [P, PACK], F32)
-        c_nth = sb("c_nth", [P, PACK], F32)
-        nc.scalar.activation(c_nth[:], c_th[:], COPY, scale=-1.0)
+            nc.vector.tensor_copy(picked_w[:, cols], x_w[:].bitcast(U32).indirect(half_list(l_offs, h)))
+        nc.scalar.copy(dealt(w1_w[:]), plain(w1_w_plain[:].bitcast(U32)))
+
+        bias = sb("bias", [P, PACK], F32)
+        minus_threshold = sb("minus_threshold", [P, PACK], F32)
+        nc.scalar.activation(minus_threshold[:], threshold[:], COPY, scale=-1.0)
         for t in range(PACK):
-            nc.scalar.activation(c_nb[:, t : t + 1], c_nth[:, t : t + 1], COPY, scale=c_sl[:, t : t + 1])
-
-        c_gk75 = sb("c_gk75", [P, PACK], F32)
-        nc.vector.tensor_scalar(c_gk75[:], c_gk[:], 0.75, None, MULT)
-
-        def product(dst, lw, ls, t, rw, rs, cols):
-            rows = slice(P * t, P * (t + 1))
-            nc.tensor.matmul_mx(out=dst[:, cols], lhsT=lw[:, rows].bitcast(FP8X4), lhsT_scale=ls[:, rows],
-                                rhs=rw[:, cols].bitcast(FP8X4), rhs_scale=rs[:, cols], start=True, stop=True)
+            nc.scalar.activation(bias[:, t : t + 1], minus_threshold[:, t : t + 1], COPY, scale=slope[:, t : t + 1])
+        z2_gain = sb("z2_gain", [P, PACK], F32)
+        nc.vector.tensor_scalar(z2_gain[:], key_gain[:], 0.75, None, MULT)
 
         y_ps = [bank(t, "y_ps%d" % t) for t in range(PACK)]
         y = [sb("y%d" % t, [P, 2 * S], F32) for t in range(PACK)]
-        ys = [sb("ys%d" % t, [P, 2 * S], F32)[:] for t in range(2)]
+        scaled_y = [sb("scaled_y%d" % t, [P, 2 * S], F32)[:] for t in range(2)]
         sg = [sb("sg%d" % t, [P, S], F32) for t in range(PACK)]
         for cols, dst in zip(halves, (y_ps[0], bank(PACK, "y_ps0_right"))):
-            product(dst, w1w, w1s, 0, xq_w, xq_s, cols)
+            product(dst[:, cols], w1_w, w1_s, 0, picked_w, picked_s, cols)
             nc.scalar.copy(y[0][:, cols], dst[:, cols])
         for t in range(1, PACK):
-            product(y_ps[t], w1w, w1s, t, xq_w, xq_s, slice(0, S))
-            if t < 2:
-                nc.scalar.copy(y[t][:, 0:S], y_ps[t][:])
-            else:
-                nc.vector.tensor_copy(y[t][:, 0:S], y_ps[t][:])
+            product(y_ps[t][:], w1_w, w1_s, t, picked_w, picked_s, slice(0, S))
+            copy_out = nc.scalar.copy if t == 1 else nc.vector.tensor_copy
+            copy_out(y[t][:, 0:S], y_ps[t][:])
+
+        cand_w = sb("cand_w", [P, S], U32)
+        cand_s = sb("cand_s", [P, S], U8)
+        nc.vector.tensor_copy(dealt(cand_w[:]), x_w[:].bitcast(U32).indirect(l_cand[:]))
+        nc.vector.tensor_copy(dealt(cand_s[:]), x_s[:].indirect(l_cand[:]))
 
         st_all = sb("st_all", [P, PACK, S], F32)
-        st2 = sb("st_n2", [P, PACK, S], F32)
-        cw = sb("cw", [P, S], U32)
-        cs = sb("cs", [P, S], U8)
-        kw = sb("kw", [P, S], U32)
-        ks_d = sb("ks_d", [P, S], U8)
-        nc.vector.tensor_copy(dealt(cw[:]), xw[:].bitcast(U32).indirect(l_cand[:]))
-        nc.vector.tensor_copy(dealt(cs[:]), xs[:].indirect(l_cand[:]))
+        st_n2 = sb("st_n2", [P, PACK, S], F32)
+        key_w = sb("key_w", [P, S], U32)
+        key_s_by_run = sb("key_s_by_run", [P, S], U8)
+        key_steps = [(d_s[:], U8, key_s_by_run, h) for h in range(2)] + [(d_w[:].bitcast(U32), U32, key_w, h) for h in range(2)]
         st = []
-        for t in range(PACK):
+        for t, (table, dtype, dst, h) in enumerate(key_steps):
             col = slice(t, t + 1)
-            nc.scalar.activation(sg[t][:], y[t][:].indirect(l_n1[:]), SIGMOID, bias=c_nb[:, col], scale=c_sl[:, col])
-            h = t % 2
-            part = l_k1[:, 16 * h : 16 * (h + 1)]
-            places = slice(64 * h, 64 * (h + 1))
-            if t < 2:
-                picked = sb("ks_g%d" % h, [P, HALF], U8, tag="st%d" % t)
-                nc.vector.tensor_copy(picked[:], ds[:].indirect(part))
-                nc.vector.tensor_copy(dealt(ks_d[:])[:, places, :], as_read(picked[:]))
-            else:
-                picked = sb("kw_g%d" % h, [P, HALF], U32, tag="st%d" % t)
-                nc.vector.tensor_copy(picked[:], dw[:].bitcast(U32).indirect(part))
-                nc.vector.tensor_copy(dealt(kw[:])[:, places, :], as_read(picked[:]))
-            if t == 1:
-                for j, src in enumerate((0, 1, 16, 17)):
-                    nc.sync.dma_start(ks[j:P:32, :].bitcast(I32), ks_d[src:P:32, :].bitcast(I32))
-            st.append(sb("st%d" % t, [P, (2 if t < 3 else 4) * S], F32))
-            nc.vector.scalar_tensor_tensor(st[t][:, 0:S], y_ps[t][:] if t else y[t][:, 0:S], c_gs[:, col], sg[t][:], MULT, MULT)
-            if t < PACK - 1:
-                nc.sync.dma_start(st_all[:, t, :], st[t][:, 0:S])
-            else:
-                nc.vector.tensor_copy(st_all[:, t, :], st[t][:, 0:S])
+            last = t == PACK - 1
+            nc.scalar.activation(sg[t][:], y[t][:].indirect(l_n1[:]), SIGMOID, bias=bias[:, col], scale=slope[:, col])
+            key_part = sb("key_part%d" % t, [P, HALF], dtype, tag="st%d" % t)
+            nc.vector.tensor_copy(key_part[:], table.indirect(half_list(l_k1, h)))
+            nc.vector.tensor_copy(dealt(dst[:])[:, HALF // PACK * h : HALF // PACK * (h + 1), :], plain(key_part[:]))
+            if dst is key_s_by_run and h == 1:
+                for j, src in enumerate((0, 1, GROUP, GROUP + 1)):
+                    nc.sync.dma_start(key_s[j:P:QUADRANT, :].bitcast(I32), key_s_by_run[src:P:QUADRANT, :].bitcast(I32))
+            st.append(sb("st%d" % t, [P, (4 if last else 2) * S], F32))
+            y_values = y_ps[t][:] if t > 0 else y[0][:, 0:S]
+            nc.vector.scalar_tensor_tensor(st[t][:, 0:S], y_values, z_gain[:, col], sg[t][:], MULT, MULT)
+            gather_tiles = nc.vector.tensor_copy if last else nc.sync.dma_start
+            gather_tiles(st_all[:, t, :], st[t][:, 0:S])
         for t in range(2):
-            nc.vector.tensor_scalar(ys[t][:, 0:S], y[t][:, 0:S], c_gk75[:, t : t + 1], None, MULT)
+            nc.vector.tensor_scalar(scaled_y[t][:, 0:S], y[t][:, 0:S], z2_gain[:, t : t + 1], None, MULT)
         for t in range(PACK):
-            nc.scalar.activation(st2[:, t, :], st[t][:].indirect(l_n2[:]), COPY, scale=0.5)
-        ys_late = sb("ys_late", [P, 3 * S], F32, tag="sg3")
-        ys = ys + [ys_late[:, 0 : 2 * S], ys_late[:, S : 3 * S]]
+            nc.scalar.activation(st_n2[:, t, :], st[t][:].indirect(l_n2[:]), COPY, scale=0.5)
+        scaled_y_late = sb("scaled_y_late", [P, 3 * S], F32, tag="sg3")
+        scaled_y = scaled_y + [scaled_y_late[:, 0 : 2 * S], scaled_y_late[:, S : 3 * S]]
 
-        def woven_src(ap):
-            return ap.rearrange("p t (c i) -> p c t i", i=4)
-
-        def woven_dst(ap):
-            return ap.rearrange("p (c i) t -> p c t i", i=4)
-
-        def quantise(words, scales, src, cols):
-            nc.vector.quantize_mx(out=words[:, cols].bitcast(FP8X4), scales=scales[:, cols],
-                                  in_=src[:, cols, :].rearrange("p c t -> p (c t)"))
-
-        z_bf = sb("z_bf", [P, S, PACK], BF16)
+        z_woven = sb("z_woven", [P, S, PACK], BF16)
         z_w = sb("z_w", [P, S], U32)
         z_s = sb("z_s", [P, S], U8)
-        nc.vector.tensor_tensor(woven_dst(z_bf[:]), woven_src(st_all[:]), woven_src(st2[:]), SUB)
+        weave_difference(z_woven, st_all, st_n2, slice(0, S))
 
-        spare = [st[3][:, S * j : S * (j + 1)] for j in (1, 2, 3, 0)] + [sb("g_%d" % j, [P, S], F32)[:] for j in range(4)]
-        g3, g5 = spare[0::2], spare[1::2]
-        pp, qq = st_all, st2
+        fetched = [st[PACK - 1][:, S * j : S * (j + 1)] for j in (1, 2, 3, 0)]
+        fetched = fetched + [sb("fetched%d" % j, [P, S], F32)[:] for j in range(PACK)]
+        y_n3, y_n5 = fetched[0::2], fetched[1::2]
+        left, right = st_all, st_n2
         a_ps = [bank(PACK + t, "a_ps%d" % t) for t in range(PACK)]
         for t in range(PACK):
             if t >= 2:
-                nc.scalar.activation(ys[t][:, 0:S], y[t][:, 0:S], COPY, scale=c_gk75[:, t : t + 1])
-            nc.scalar.activation(g3[t], ys[t].indirect(l_n3[:]), COPY)
-            nc.scalar.activation(g5[t], ys[t].indirect(l_n5[:]), COPY)
-            nc.vector.tensor_tensor(pp[:, t, :], y[t][:].indirect(l_n4[:]), g3[t], MULT)
+                nc.scalar.activation(scaled_y[t][:, 0:S], y[t][:, 0:S], COPY, scale=z2_gain[:, t : t + 1])
+            nc.scalar.activation(y_n3[t], scaled_y[t].indirect(l_n3[:]), COPY)
+            nc.scalar.activation(y_n5[t], scaled_y[t].indirect(l_n5[:]), COPY)
+            nc.vector.tensor_tensor(left[:, t, :], y[t][:].indirect(l_n4[:]), y_n3[t], MULT)
             if t == 0:
-                quantise(z_w, z_s, z_bf, slice(0, S))
+                quantise(z_w, z_s, z_woven, slice(0, S))
                 for u in range(PACK):
-                    product(a_ps[u], cw, cs, u, z_w, z_s, slice(0, S))
-            nc.vector.tensor_tensor(qq[:, t, :], y[t][:].indirect(l_n6[:]), g5[t], MULT)
+                    product(a_ps[u][:], cand_w, cand_s, u, z_w, z_s, slice(0, S))
+            nc.vector.tensor_tensor(right[:, t, :], y[t][:].indirect(l_n6[:]), y_n5[t], MULT)
 
-        res = [sb("res%d" % t, [P, S], F32) for t in range(PACK)]
-        g7 = [sb("g7_%d" % t, [P, W], F32) for t in range(PACK)]
+        result = [sb("result%d" % t, [P, S], F32) for t in range(PACK)]
+        a_n7 = [sb("a_n7_%d" % t, [P, W], F32) for t in range(PACK)]
         for t in range(PACK):
-            nc.scalar.activation(res[t][:], a_ps[t][:], COPY, scale=0.0625)
-            nc.scalar.activation(g7[t][:], res[t][:].indirect(l_n7[:]), COPY, scale=-0.5)
+            nc.scalar.activation(result[t][:], a_ps[t][:], COPY, scale=SCORE_SCALE)
+            nc.scalar.activation(a_n7[t][:], result[t][:].indirect(l_n7[:]), COPY, scale=-0.5)
 
-        z2_bf = sb("z2_bf", [P, S, PACK], BF16)
+        z2_woven = sb("z2_woven", [P, S, PACK], BF16)
         z2_w = sb("z2_w", [P, S], U32)
         z2_s = sb("z2_s", [P, S], U8)
-        b_ps = [[bank(2 * h + u, "b_ps%d%d" % (h, u)) for u in range(2)] for h in range(2)]
+        b_ps = [[bank(2 * h + odd, "b_ps%d%d" % (h, odd)) for odd in range(2)] for h in range(2)]
         b = [sb("b%d" % t, [P, S], F32) for t in range(PACK)]
         for cols in halves:
-            nc.vector.tensor_tensor(woven_dst(z2_bf[:, cols, :]), woven_src(pp[:, :, cols]), woven_src(qq[:, :, cols]), SUB)
+            weave_difference(z2_woven, left, right, cols)
         for h, cols in enumerate(halves):
-            quantise(z2_w, z2_s, z2_bf, cols)
+            quantise(z2_w, z2_s, z2_woven, cols)
+            places = [b_ps[h][t % 2][:, halves[t // 2]] for t in range(PACK)]
             for t in range(PACK):
-                rows = slice(P * t, P * (t + 1))
-                dst = b_ps[h][t % 2][:, HALF * (t // 2) : HALF * (t // 2 + 1)]
-                nc.tensor.matmul_mx(out=dst, lhsT=kw[:, rows].bitcast(FP8X4), lhsT_scale=ks[:, rows],
-                                    rhs=z2_w[:, cols].bitcast(FP8X4), rhs_scale=z2_s[:, cols], start=True, stop=True)
+                product(places[t], key_w, key_s, t, z2_w, z2_s, cols)
             for t in range(PACK):
-                src = b_ps[h][t % 2][:, HALF * (t // 2) : HALF * (t // 2 + 1)]
                 if h == 1 and t % 2 == 1:
-                    nc.vector.tensor_scalar(b[t][:, cols], src, 0.0625, None, MULT)
+                    nc.vector.tensor_scalar(b[t][:, cols], places[t], SCORE_SCALE, None, MULT)
                 else:
-                    nc.scalar.activation(b[t][:, cols], src, COPY, scale=0.0625)
+                    nc.scalar.activation(b[t][:, cols], places[t], COPY, scale=SCORE_SCALE)
 
-        g8 = [sb("g8_%d" % t, [P, W], F32) for t in range(PACK)]
-        stage = sb("stage", [P, PACK, S], F32)
+        b_n8 = [sb("b_n8_%d" % t, [P, W], F32) for t in range(PACK)]
+        result_all = sb("result_all", [P, PACK, S], F32)
         out_rows = out_0.rearrange("(p t) n -> p t n", t=PACK)
         for t in range(PACK):
             if t % 2 == 0:
-                nc.scalar.activation(g8[t][:], b[t][:].indirect(l_n8[:]), COPY)
+                nc.scalar.activation(b_n8[t][:], b[t][:].indirect(l_n8[:]), COPY)
             else:
-                nc.vector.tensor_tensor(g8[t][:], b[t][:].indirect(l_n8[:]), g7[t][:], ADD)
+                nc.vector.tensor_tensor(b_n8[t][:], b[t][:].indirect(l_n8[:]), a_n7[t][:], ADD)
         for t in range(PACK):
             if t % 2 == 0:
-                nc.vector.tensor_tensor(res[t][:].indirect(l_n7[:]), g8[t][:], g7[t][:], ADD)
+                nc.vector.tensor_tensor(result[t][:].indirect(l_n7[:]), b_n8[t][:], a_n7[t][:], ADD)
             else:
-                nc.scalar.activation(res[t][:].indirect(l_n7[:]), g8[t][:], COPY)
-            nc.sync.dma_start(out_rows[:, t, :], res[t][:])
+                nc.scalar.activation(result[t][:].indirect(l_n7[:]), b_n8[t][:], COPY)
+            nc.sync.dma_start(out_rows[:, t, :], result[t][:])
         for t in range(PACK):
-            if t == 1:
-                nc.scalar.copy(stage[:, t, :], res[t][:])
-            else:
-                nc.vector.tensor_copy(stage[:, t, :], res[t][:])
+            copy_tile = nc.scalar.copy if t == 1 else nc.vector.tensor_copy
+            copy_tile(result_all[:, t, :], result[t][:])
 
-        o_bf = sb("o_bf", [P, S, PACK], BF16)
-        o_w = sb("o_w", [P, S], U32)
-        o_s = sb("o_s", [P, S], U8)
-        out_words = words_of(out_1)
-        for eng_copy, cols in zip((nc.vector.tensor_copy, nc.scalar.copy), halves):
-            eng_copy(woven_dst(o_bf[:, cols, :]), woven_src(stage[:, :, cols]))
+        out_woven = sb("out_woven", [P, S, PACK], BF16)
+        out_w = sb("out_w", [P, S], U32)
+        out_s = sb("out_s", [P, S], U8)
+        for weave, cols in zip((nc.vector.tensor_copy, nc.scalar.copy), halves):
+            weave(into_woven(out_woven[:, cols, :], 4), from_tiles(result_all[:, :, cols], 4))
         for cols in halves:
-            quantise(o_w, o_s, o_bf, cols)
-            nc.sync.dma_start(out_words[:, cols], o_w[:, cols].bitcast(I32))
-        for q in range(4):
-            eng = nc.sync if q % 2 == 0 else nc.scalar
-            eng.dma_start(out_2[0, 4 * q : 4 * q + 4, :].bitcast(I32), o_s[32 * q : 32 * q + 4, :].bitcast(I32))
+            quantise(out_w, out_s, out_woven, cols)
+            nc.sync.dma_start(words_of(out_1)[:, cols], out_w[:, cols].bitcast(I32))
+        for q in range(P // QUADRANT):
+            queue = nc.sync if q % 2 == 0 else nc.scalar
+            queue.dma_start(out_2[0, 4 * q : 4 * q + 4, :].bitcast(I32), out_s[QUADRANT * q : QUADRANT * q + 4, :].bitcast(I32))

from contextlib import ExitStack

import concourse.mybir as mybir

F32 = mybir.dt.float32
BF16 = mybir.dt.bfloat16
I32 = mybir.dt.int32
U32 = mybir.dt.uint32
U16 = mybir.dt.uint16
U8 = mybir.dt.uint8
FP8X4 = mybir.dt.float8_e4m3fn_x4
MULT = mybir.AluOpType.mult
ADD = mybir.AluOpType.add
SUB = mybir.AluOpType.subtract
COPY = mybir.ActivationFunctionType.Copy
SIGMOID = mybir.ActivationFunctionType.Sigmoid

P = 128
PACK = 4
S = 512
T = 1024
G = 2048
W = 256
HALF = S // 2
GROUP = 16
QUADRANT = 32
SCORE_SCALE = 0.0625
FLOPS = 3 * 2 * S * S * S


def tile_picked_cdkeyputbehpdet_none_po_kernel(
    tc, x_words, x_scales, w1_words, w1_scales, sl, th, gs, gk, d_words, d_scales,
    offs, n1, n2, n3, n4, n5, n6, cand, k1, n7, n8, out_0, out_1, out_2,
):
    nc = tc.nc
    halves = [slice(0, HALF), slice(HALF, S)]
    with ExitStack() as ctx:
        keep = ctx.enter_context(tc.tile_pool(name="keep", bufs=1))
        psum = ctx.enter_context(tc.psum_pool(name="psum", bufs=1))

        def sb(name, shape, dtype, tag=""):
            return keep.tile(shape, dtype, name=name, tag=tag or name, align_bytes=64)

        def bank(number, name):
            return psum.tile([P, S], F32, name=name, tag="bank%d" % number)

        def load_list(name, src):
            tile = keep.tile(list(src.shape), U16, name=name)
            nc.sync.dma_start(tile[:], src)
            return tile

        def load_row_factors(name, src):
            tile = sb(name, [P, PACK], F32)
            nc.sync.dma_start(tile[:], src.rearrange("(p t) o -> p (t o)", t=PACK))
            return tile

        def load_scale_rows(dst, src):
            for q in range(P // QUADRANT):
                nc.sync.dma_start(dst[QUADRANT * q : QUADRANT * q + 4, :].bitcast(I32), src[0, 4 * q : 4 * q + 4, :].bitcast(I32))

        def words_of(dram):
            return dram[0].rearrange("p n r -> p (n r)").bitcast(I32)

        def dealt(ap):
            return ap.rearrange("p (t m) -> p m t", t=PACK)

        def plain(ap):
            return ap.rearrange("p (m t) -> p m t", t=PACK)

        def half_list(tile, h):
            columns = HALF // GROUP
            return tile[:, columns * h : columns * (h + 1)]

        def product(dst, words, scales, t, moving_words, moving_scales, cols):
            rows = slice(P * t, P * (t + 1))
            nc.tensor.matmul_mx(
                out=dst, lhsT=words[:, rows].bitcast(FP8X4), lhsT_scale=scales[:, rows],
                rhs=moving_words[:, cols].bitcast(FP8X4), rhs_scale=moving_scales[:, cols], start=True, stop=True,
            )

        def from_tiles(ap, run):
            return ap.rearrange("p t (c i) -> p c t i", i=run)

        def into_woven(ap, run):
            return ap.rearrange("p (c i) t -> p c t i", i=run)

        def weave_difference(dst, left, right, cols):
            nc.vector.tensor_tensor(into_woven(dst[:, cols, :], 2), from_tiles(left[:, :, cols], 2), from_tiles(right[:, :, cols], 2), SUB)

        def quantise(words, scales, woven, cols):
            nc.vector.quantize_mx(
                out=words[:, cols].bitcast(FP8X4), scales=scales[:, cols],
                in_=woven[:, cols, :].rearrange("p c t -> p (c t)"),
            )

        warm_in = sb("warm_in", [P, 1], F32)
        warm_out = sb("warm_out", [P, 1], F32)
        nc.vector.memset(warm_in[:], 0.0)
        nc.scalar.activation(warm_out[:], warm_in[:], SIGMOID)

        x_s = sb("x_s", [P, T], U8)
        w1_s_plain = sb("w1_s_plain", [P, S], U8)
        d_s = sb("d_s", [P, G], U8)
        key_s = sb("key_s", [P, S], U8)
        nc.gpsimd.memset(x_s[:].bitcast(I32), 0)
        nc.vector.memset(w1_s_plain[:].bitcast(I32), 0)
        nc.vector.memset(d_s[:].bitcast(I32), 0)
        nc.vector.memset(key_s[:].bitcast(I32), 0)

        x_w = sb("x_w", [P, T], I32)
        w1_w_plain = sb("w1_w_plain", [P, S], I32)
        d_w = sb("d_w", [P, G], I32)
        l_offs = load_list("l_offs", offs)
        nc.sync.dma_start(w1_w_plain[:], words_of(w1_words))
        slope = load_row_factors("slope", sl)
        threshold = load_row_factors("threshold", th)
        load_scale_rows(x_s, x_scales)
        nc.sync.dma_start(x_w[:], words_of(x_words))
        load_scale_rows(w1_s_plain, w1_scales)
        l_cand = load_list("l_cand", cand)
        l_n1 = load_list("l_n1", n1)
        l_k1 = load_list("l_k1", k1)
        for e in range(2):
            nc.sync.dma_start(d_s[e:P:GROUP, :].bitcast(I32), d_scales[0, e:16:2, :].bitcast(I32))
        z_gain = load_row_factors("z_gain", gs)
        key_gain = load_row_factors("key_gain", gk)
        nc.sync.dma_start(d_w[:], words_of(d_words))
        l_n2 = load_list("l_n2", n2)
        l_n3 = load_list("l_n3", n3)
        l_n5 = load_list("l_n5", n5)
        l_n4 = load_list("l_n4", n4)
        l_n6 = load_list("l_n6", n6)
        l_n7 = load_list("l_n7", n7)
        l_n8 = load_list("l_n8", n8)

        picked_s = sb("picked_s", [P, S], U8)
        picked_w = sb("picked_w", [P, S], U32)
        w1_s = sb("w1_s", [P, S], U8)
        w1_w = sb("w1_w", [P, S], U32)
        nc.vector.tensor_copy(picked_s[:], x_s[:].indirect(l_offs[:]))
        nc.vector.tensor_copy(dealt(w1_s[:]), plain(w1_s_plain[:]))
        for h, cols in enumerate(halves):
            nc.vector.tensor_copy(picked_w[:, cols], x_w[:].bitcast(U32).indirect(half_list(l_offs, h)))
        nc.scalar.copy(dealt(w1_w[:]), plain(w1_w_plain[:].bitcast(U32)))

        bias = sb("bias", [P, PACK], F32)
        minus_threshold = sb("minus_threshold", [P, PACK], F32)
        nc.scalar.activation(minus_threshold[:], threshold[:], COPY, scale=-1.0)
        for t in range(PACK):
            nc.scalar.activation(bias[:, t : t + 1], minus_threshold[:, t : t + 1], COPY, scale=slope[:, t : t + 1])
        z2_gain = sb("z2_gain", [P, PACK], F32)
        nc.vector.tensor_scalar(z2_gain[:], key_gain[:], 0.75, None, MULT)

        y_ps = [bank(t, "y_ps%d" % t) for t in range(PACK)]
        y = [sb("y%d" % t, [P, 2 * S], F32) for t in range(PACK)]
        scaled_y = [sb("scaled_y%d" % t, [P, 2 * S], F32)[:] for t in range(2)]
        sg = [sb("sg%d" % t, [P, S], F32) for t in range(PACK)]
        for cols, dst in zip(halves, (y_ps[0], bank(PACK, "y_ps0_right"))):
            product(dst[:, cols], w1_w, w1_s, 0, picked_w, picked_s, cols)
            nc.scalar.copy(y[0][:, cols], dst[:, cols])
        for t in range(1, PACK):
            product(y_ps[t][:], w1_w, w1_s, t, picked_w, picked_s, slice(0, S))
            copy_out = nc.scalar.copy if t == 1 else nc.vector.tensor_copy
            copy_out(y[t][:, 0:S], y_ps[t][:])

        cand_w = sb("cand_w", [P, S], U32)
        cand_s = sb("cand_s", [P, S], U8)
        nc.vector.tensor_copy(dealt(cand_w[:]), x_w[:].bitcast(U32).indirect(l_cand[:]))
        nc.vector.tensor_copy(dealt(cand_s[:]), x_s[:].indirect(l_cand[:]))

        st_all = sb("st_all", [P, PACK, S], F32)
        st_n2 = sb("st_n2", [P, PACK, S], F32)
        key_w = sb("key_w", [P, S], U32)
        key_s_by_run = sb("key_s_by_run", [P, S], U8)
        key_steps = [(d_s[:], U8, key_s_by_run, h) for h in range(2)] + [(d_w[:].bitcast(U32), U32, key_w, h) for h in range(2)]
        st = []
        for t, (table, dtype, dst, h) in enumerate(key_steps):
            col = slice(t, t + 1)
            last = t == PACK - 1
            nc.scalar.activation(sg[t][:], y[t][:].indirect(l_n1[:]), SIGMOID, bias=bias[:, col], scale=slope[:, col])
            key_part = sb("key_part%d" % t, [P, HALF], dtype, tag="st%d" % t)
            nc.vector.tensor_copy(key_part[:], table.indirect(half_list(l_k1, h)))
            nc.vector.tensor_copy(dealt(dst[:])[:, HALF // PACK * h : HALF // PACK * (h + 1), :], plain(key_part[:]))
            if dst is key_s_by_run and h == 1:
                for j, src in enumerate((0, 1, GROUP, GROUP + 1)):
                    nc.sync.dma_start(key_s[j:P:QUADRANT, :].bitcast(I32), key_s_by_run[src:P:QUADRANT, :].bitcast(I32))
            st.append(sb("st%d" % t, [P, (4 if last else 2) * S], F32))
            y_values = y_ps[t][:] if t > 0 else y[0][:, 0:S]
            nc.vector.scalar_tensor_tensor(st[t][:, 0:S], y_values, z_gain[:, col], sg[t][:], MULT, MULT)
            gather_tiles = nc.vector.tensor_copy if last else nc.sync.dma_start
            gather_tiles(st_all[:, t, :], st[t][:, 0:S])
        for t in range(2):
            nc.vector.tensor_scalar(scaled_y[t][:, 0:S], y[t][:, 0:S], z2_gain[:, t : t + 1], None, MULT)
        for t in range(PACK):
            nc.scalar.activation(st_n2[:, t, :], st[t][:].indirect(l_n2[:]), COPY, scale=0.5)
        scaled_y_late = sb("scaled_y_late", [P, 3 * S], F32, tag="sg3")
        scaled_y = scaled_y + [scaled_y_late[:, 0 : 2 * S], scaled_y_late[:, S : 3 * S]]

        z_woven = sb("z_woven", [P, S, PACK], BF16)
        z_w = sb("z_w", [P, S], U32)
        z_s = sb("z_s", [P, S], U8)
        weave_difference(z_woven, st_all, st_n2, slice(0, S))

        fetched = [st[PACK - 1][:, S * j : S * (j + 1)] for j in (1, 2, 3, 0)]
        fetched = fetched + [sb("fetched%d" % j, [P, S], F32)[:] for j in range(PACK)]
        y_n3, y_n5 = fetched[0::2], fetched[1::2]
        left, right = st_all, st_n2
        a_ps = [bank(PACK + t, "a_ps%d" % t) for t in range(PACK)]
        for t in range(PACK):
            if t >= 2:
                nc.scalar.activation(scaled_y[t][:, 0:S], y[t][:, 0:S], COPY, scale=z2_gain[:, t : t + 1])
            nc.scalar.activation(y_n3[t], scaled_y[t].indirect(l_n3[:]), COPY)
            nc.scalar.activation(y_n5[t], scaled_y[t].indirect(l_n5[:]), COPY)
            nc.vector.tensor_tensor(left[:, t, :], y[t][:].indirect(l_n4[:]), y_n3[t], MULT)
            if t == 0:
                quantise(z_w, z_s, z_woven, slice(0, S))
                for u in range(PACK):
                    product(a_ps[u][:], cand_w, cand_s, u, z_w, z_s, slice(0, S))
            nc.vector.tensor_tensor(right[:, t, :], y[t][:].indirect(l_n6[:]), y_n5[t], MULT)

        result = [sb("result%d" % t, [P, S], F32) for t in range(PACK)]
        a_n7 = [sb("a_n7_%d" % t, [P, W], F32) for t in range(PACK)]
        for t in range(PACK):
            nc.scalar.activation(result[t][:], a_ps[t][:], COPY, scale=SCORE_SCALE)
            nc.scalar.activation(a_n7[t][:], result[t][:].indirect(l_n7[:]), COPY, scale=-0.5)

        z2_woven = sb("z2_woven", [P, S, PACK], BF16)
        z2_w = sb("z2_w", [P, S], U32)
        z2_s = sb("z2_s", [P, S], U8)
        b_ps = [[bank(2 * h + odd, "b_ps%d%d" % (h, odd)) for odd in range(2)] for h in range(2)]
        b = [sb("b%d" % t, [P, S], F32) for t in range(PACK)]
        for cols in halves:
            weave_difference(z2_woven, left, right, cols)
        for h, cols in enumerate(halves):
            quantise(z2_w, z2_s, z2_woven, cols)
            places = [b_ps[h][t % 2][:, halves[t // 2]] for t in range(PACK)]
            for t in range(PACK):
                product(places[t], key_w, key_s, t, z2_w, z2_s, cols)
            for t in range(PACK):
                if h == 1 and t % 2 == 1:
                    nc.vector.tensor_scalar(b[t][:, cols], places[t], SCORE_SCALE, None, MULT)
                else:
                    nc.scalar.activation(b[t][:, cols], places[t], COPY, scale=SCORE_SCALE)

        b_n8 = [sb("b_n8_%d" % t, [P, W], F32) for t in range(PACK)]
        result_all = sb("result_all", [P, PACK, S], F32)
        out_rows = out_0.rearrange("(p t) n -> p t n", t=PACK)
        for t in range(PACK):
            if t % 2 == 0:
                nc.scalar.activation(b_n8[t][:], b[t][:].indirect(l_n8[:]), COPY)
            else:
                nc.vector.tensor_tensor(b_n8[t][:], b[t][:].indirect(l_n8[:]), a_n7[t][:], ADD)
        for t in range(PACK):
            if t % 2 == 0:
                nc.vector.tensor_tensor(result[t][:].indirect(l_n7[:]), b_n8[t][:], a_n7[t][:], ADD)
            else:
                nc.scalar.activation(result[t][:].indirect(l_n7[:]), b_n8[t][:], COPY)
            nc.sync.dma_start(out_rows[:, t, :], result[t][:])
        for t in range(PACK):
            copy_tile = nc.scalar.copy if t == 1 else nc.vector.tensor_copy
            copy_tile(result_all[:, t, :], result[t][:])

        out_woven = sb("out_woven", [P, S, PACK], BF16)
        out_w = sb("out_w", [P, S], U32)
        out_s = sb("out_s", [P, S], U8)
        for weave, cols in zip((nc.vector.tensor_copy, nc.scalar.copy), halves):
            weave(into_woven(out_woven[:, cols, :], 4), from_tiles(result_all[:, :, cols], 4))
        for cols in halves:
            quantise(out_w, out_s, out_woven, cols)
            nc.sync.dma_start(words_of(out_1)[:, cols], out_w[:, cols].bitcast(I32))
        for q in range(P // QUADRANT):
            queue = nc.sync if q % 2 == 0 else nc.scalar
            queue.dma_start(out_2[0, 4 * q : 4 * q + 4, :].bitcast(I32), out_s[QUADRANT * q : QUADRANT * q + 4, :].bitcast(I32))
